import numpy as np, ml_dtypes
CORES = [10,34,74,98]
N = 4
BF = ml_dtypes.bfloat16
def gentries(a):
    return np.ascontiguousarray(a.reshape(8, 16, -1).transpose(0, 2, 1)).reshape(8, -1)
def gtable(e):
    e = np.asarray(e); return np.ascontiguousarray(e.reshape(8, -1, 16).transpose(0, 2, 1)).reshape(128, -1).astype(np.int32)
R, F, C, D, B = 16384, 4096, 1024, 2, 1 << 20
def passing(at, lim):
    a0 = at[:, 0].reshape(8, R); l = lim.reshape(8, 2)
    return (a0 >= l[:, :1]) & (a0 <= l[:, 1:])
def dims(rng, m, w, first=None):
    lo = rng.integers(-(B >> 1), B >> 2, (8, 1)); hi = lo + w[:, None]; z = rng.random((8, R))
    if first is not None: z[np.arange(8), first] = -1
    ok = np.argsort(np.argsort(z, 1), 1) < m[:, None]
    out = np.where(rng.random((8, R)) < 0.5, rng.integers(1 - B, lo, (8, R)), rng.integers(hi + 1, B, (8, R)))
    return lo, hi, ok, np.where(ok, rng.integers(lo, hi + 1, (8, R)), out)
def living(n, z):
    return np.argsort(np.argsort(z, 1), 1) < n[:, None]
def facts(rng, ok, live, p, where, e=1):
    m = np.sum(ok, axis=1)[:, None]; o = np.argsort(~ok, 1, kind="stable")
    bad = rng.random((N, 8, F)) < p; np.put_along_axis(bad, where, True, 1); bad = bad & ~live[:, None]
    k = np.where(bad, R - m, m); j = np.minimum((rng.random((N, 8, F)) ** e * k).astype(np.int64), k - 1)
    return o[np.arange(8)[:, None], j + np.where(bad, m, 0)]
def pack(lo, hi, v, rest, fk, me):
    rest[:, 0] = v
    return {"at": np.ascontiguousarray(rest.reshape(N, D, 16, R).transpose(0, 2, 1, 3)).reshape(N, 16, D * R).astype(np.int32),
            "lim": np.concatenate([lo, hi], 1).reshape(N, 1, 2 * D).astype(np.int32), "fk": np.stack([gtable(x) for x in fk]), "me": me.reshape(N, 1, F).astype(np.int32)}
def whole(rng, *shape):
    return rng.integers(1 - B, B, shape)
def setup_inputs(rng):
    lo, hi, ok, v = dims(rng, rng.integers(R // 4, 3 * R // 4, 8), rng.integers(B >> 6, B >> 2, 8))
    live = living(rng.integers(C // 4, C, N), rng.random((N, F)))
    return pack(lo, hi, v, whole(rng, 8, 16, R), facts(rng, ok, live, 0.15, rng.integers(0, 8, (N, 1, F))), whole(rng, N, F))
def setup_inputs_full(rng):
    lo, hi, ok, v = dims(rng, rng.integers(R // 4, 3 * R // 4, 8), rng.integers(B >> 6, B >> 2, 8))
    n = np.full(N, C); n[rng.integers(0, N)] = 1; z = rng.random((N, F)); z[:, 0] = -1; z[:, -1] = -2
    return pack(lo, hi, v, whole(rng, 8, 16, R), facts(rng, ok, living(n, z), 0.3, rng.integers(0, 8, (N, 1, F))), whole(rng, N, F))
def setup_inputs_ends(rng):
    w = np.where(rng.permutation(8) < 3, 0, rng.integers(1, 1000, 8))
    lo, hi, ok, v = dims(rng, rng.integers(R // 4, 3 * R // 4, 8), w); h = rng.random((8, R)) < 0.5
    v = np.where(ok, np.where(h, lo, hi), np.where(h, lo - 1, hi + 1)); j = np.arange(F)
    live = living(rng.integers(C // 4, C + 1, N), np.minimum(j, F - 1 - j)[None] + np.zeros((N, 1)))
    return pack(lo, hi, v, whole(rng, 8, 16, R), facts(rng, ok, live, 0.1, rng.integers(0, 8, (N, 1, F))), whole(rng, N, F))
def setup_inputs_alike(rng):
    m = np.where(rng.permutation(8) < 4, 1, R - 1)
    lo, hi, ok, v = dims(rng, m, rng.integers(0, B >> 2, 8), np.where(rng.random(8) < 0.5, 0, R - 1))
    live = living(rng.integers(C // 4, C + 1, N), rng.random((N, F))); fk = facts(rng, ok, live, 0.1, rng.integers(0, 8, (N, 1, F)))
    q = rng.integers(0, N); s = np.flatnonzero(live[q]); fk[q][:, s] = fk[q][:, s[:1]]
    return pack(lo, hi, v, whole(rng, 8, 16, R), fk, whole(rng, N, F))
def setup_inputs_near(rng):
    lo, hi, ok, v = dims(rng, rng.integers(R // 4, 3 * R // 4, 8), rng.integers(B >> 6, B >> 2, 8))
    where = np.where(rng.random((N, 1, 1)) < 0.5, rng.integers(0, 8, (N, 1, 1)), rng.integers(0, 8, (N, 1, F)))
    live = living(rng.integers(C // 4, C + 1, N), rng.random((N, F))); sg = rng.choice(np.array([-1, 1]), (1, 16, 1))
    rest = sg * (B - 1 - rng.integers(0, 50, (8, 16, R))); me = rng.choice(np.array([-1, 1]), (N, 1)) * (B - 1 - rng.integers(0, 50, (N, F)))
    return pack(lo, hi, v, rest, facts(rng, ok, live, 0.0, where), me)
def setup_inputs_spread(rng):
    lo, hi, ok, v = dims(rng, np.maximum(1, R >> rng.integers(1, 10, 8)), 1 << rng.integers(0, 18, 8))
    live = living(np.maximum(1, C >> rng.integers(0, 6, N)), rng.random((N, F)))
    rest = whole(rng, 8, 16, R) >> rng.integers(0, 20, (8, 16, R)); me = whole(rng, N, F) >> rng.integers(0, 20, (N, F))
    return pack(lo, hi, v, rest, facts(rng, ok, live, rng.random((1, 8, 1)), rng.integers(0, 8, (N, 1, F)), 4), me)
def check_inputs(d):
    bad = [k for k in ("at", "lim", "me") if not ((d[k] > -B) & (d[k] < B)).all()]
    if not ((d["fk"] >= 0) & (d["fk"] < R)).all(): return bad + ["fk"]
    ok = passing(d["at"], d["lim"]); g = np.arange(8)[:, None]
    n = [int(np.sum(np.all(ok[g, gentries(a)], axis=0))) for a in d["fk"]]
    return bad + ([] if min(n) >= 1 and max(n) <= C else ["survivors"])
def reference(at, lim, fk, me):
    y = np.zeros((N, 16, C + 1), np.int64); ok = passing(at, lim); g = np.arange(8)[:, None]
    a = np.ascontiguousarray(at.reshape(N, 16, D, R).transpose(0, 2, 1, 3)).reshape(8, 16, R).astype(np.int64)
    for r in range(N):
        k = gentries(fk[r]); s = np.flatnonzero(np.all(ok[g, k], axis=0)); n = len(s)
        y[r, :, :n] = me[r, 0][s][None]
        for d in range(8): y[r, :, :n] += a[d][:, k[d, s]]
        y[r, :, C] = n
    return {"y": np.asarray(y, np.float32)}

@@ -1,0 +1,332 @@
+from concourse.bass import DstId, RemoteDMATransfer
+from concourse.mybir import AluOpType, ActivationFunctionType
+
+SCRATCH = {"fl": ("dram", [4, 128, 256], "bfloat16")}
+for _t, _l in {
+    "int32": "A0:256 LM:4 FK:256 HI:256 LO:256 ME:32 MR:32 J0:16 J:16 Tab:8208 OFF:32",
+    "uint16": "FKU:256 POS:32 KS:128 K0:128 K1:128 K2:128 K3:128",
+    "bfloat16": "FL:256 G:4096 HB:256 LOB:256 X:512 MB:96 MT:128 XM:512 SC:1664 SCM:1664 SELP:16 ONES:128 LT:128 KB:128 "
+                "PM:128 PMB:128 IDN:128 KH0:64 KH1:64 KH2:64 KH3:64 HM:128 SH0:128 SH1:128 SL0:128 SL1:128 "
+                "SE0:128 SE1:128 SE2:128 SE3:128 Z:136 SV:32 E:32 win:16384",
+    "float32": "LMF:4 E2:128 ONEF:128 I5:136 DD:32 SMA:32 PERM:128 W0:8 DN:32 "
+               "G0:512 G1:512 G2:512 G3:512 P0:128 P1:128 P2:128 P3:128 R0:128 R1:128 R2:128 R3:128 M1:128 CT:2 YF:128",
+}.items():
+    for _x in _l.split():
+        SCRATCH[_x.split(":")[0]] = ("sbuf", [128, int(_x.split(":")[1])], _t)
+for _b in range(8):
+    SCRATCH["B%d" % _b] = ("psum", [128, 512], "float32")
+SEMAPHORES = (["q_v", "q_s", "q_t", "q_g", "lf", "lk", "lp", "gi"]
+              + ["%s%d" % (a, i) for a in ("fl", "kk", "ps", "rl", "dz") for i in range(4)]
+              + ["d_" + n for n in ("lim", "at0", "fk", "me", "ct", "y")] + ["tb%d" % i for i in range(16)])
+
+
+def rank_program(g, core, T, topo):
+    rank = T.rank_of(core)
+    if rank is None:
+        return
+    A = AluOpType
+    COPY = ActivationFunctionType.Copy
+    eng = {"v": g.vector, "s": g.scalar, "t": g.tensor, "g": g, "y": g.sync}
+    seen = {e: {} for e in eng}
+    total = {}
+    know = {}
+    lastw, reads_of, bank_of = {}, {}, {}
+
+    def need(e, toks):
+        for s, v in sorted(toks):
+            if seen[e].get(s, 0) < v:
+                eng[e].wait_ge(T.sem[s], v)
+                for s2, v2 in know.get((s, v), {}).items():
+                    seen[e][s2] = max(seen[e].get(s2, 0), v2)
+                seen[e][s] = max(seen[e].get(s, 0), v)
+
+    def deps(e, reads, writes=(), banks=()):
+        d = {}
+
+        def put(tok):
+            d[tok[0]] = max(d.get(tok[0], 0), tok[1])
+        for r in reads:
+            for t in lastw.get(r, []):
+                put(t)
+        for w in writes:
+            for t in lastw.get(w, []) + reads_of.get(w, []):
+                put(t)
+        for b in banks:
+            if b in bank_of and bank_of[b][0] != e:
+                put(bank_of[b][1])
+        need(e, d.items())
+
+    def done(e, tok, reads, writes, banks):
+        know[tok] = dict(seen[e])
+        for r in reads:
+            reads_of.setdefault(r, []).append(tok)
+        for w in writes:
+            lastw[w] = [tok]
+            reads_of[w] = []
+        for b in banks:
+            bank_of[b] = (e, tok)
+
+    def op(e, fn, reads=(), writes=(), banks=(), join=False):
+        deps(e, reads, () if join else writes, banks)
+        s = "q_" + e
+        total[s] = total.get(s, 0) + 1
+        fn().then_inc(T.sem[s], 1)
+        done(e, (s, total[s]), reads, writes, banks)
+
+    def dma(e, out, in_, sem, reads=(), writes=()):
+        deps(e, reads, writes, ())
+        total[sem] = total.get(sem, 0) + 16
+        eng[e].dma_start(out, in_).then_inc(T.sem[sem], 16)
+        done(e, (sem, total[sem]), reads, writes, ())
+
+    def arrives(name, sem, n):
+        lastw[name] = [(sem, n)]
+        total[sem] = n
+
+    peers = [r for r in range(4) if r != rank]
+    peers.sort(key=lambda r: not topo.same_plane(topo.chip(core), topo.chip(T.cores[r])))
+
+    def n_eng(r):
+        return len(topo.engines(core, T.cores[r]))
+
+    def dst(r):
+        rid, pid, _ = topo.addr(T.cores[r])
+        return DstId(rid=rid, pnc=pid)
+
+    for r in peers:
+        n = len(topo.engines(T.cores[r], core))
+        arrives("fl%d" % r, "fl%d" % r, n)
+        arrives("K%d" % r, "kk%d" % r, n)
+        arrives("P%d" % r, "ps%d" % r, n)
+
+    V, S, P = g.vector, g.scalar, g.tensor
+
+    def mm(bank, c0, c1, lhs, rhs, a, z, reads, name, p0=0, p1=128, step=1):
+        op("t", lambda: P.matmul(T["B%d" % bank][p0:p1, c0:c1:step], lhs, rhs, a, z), reads, [name], [bank], join=True)
+
+    def select(out, in_, pattern, how, base, reads, writes, fill=0.0):
+        op("g", lambda: g.affine_select(out, in_, pattern, how, fill, base, -1), reads, writes)
+
+    dma("y", T.LM[0:2, 0:2], T.lim[:], "d_lim", (), ["LM"])
+    dma("y", T.A0[:], T.at[0:1, :], "d_at0", (), ["A0"])
+    dma("y", T.FK[:], T.fk[:], "d_fk", (), ["FK"])
+    dma("y", T.ME[:, 0:16], T.me[0:1, 0:2048], "d_me", (), ["MEa"])
+    dma("y", T.ME[:, 16:32], T.me[0:1, 2048:4096], "d_me", (), ["MEb"])
+
+    def table(i):
+        c, e, h, x = 4096 * (i % 2), i // 2 % 2, i // 4 % 2, i // 8
+        p, s = 64 * e + 32 * h + 16 * x, 16384 * e + 8192 * h + c
+        dma("y", T.Tab[p:p + 16, 8 + c:8 + c + 4096], T.at[:, s:s + 4096], "tb%d" % i, (), ["Tab%d" % i])
+
+    def fill(k):
+        c = 5120 + 1024 * k
+        dma("y", T.win[:, c:c + 1024], T.win[:, 0:1024], "dz%d" % k, ["win0"], ["win%d" % (5 + k)])
+
+    op("v", lambda: V.memset(T.ONEF[:], 1.0), (), ["ONEF"])
+    op("v", lambda: V.memset(T.win[:, 0:1024], 0.0), (), ["win0"])
+    op("v", lambda: V.memset(T.ONES[:], 1.0), (), ["ONES"])
+    fill(0)
+    fill(1)
+    op("s", lambda: S.activation(T.win[:, 1024:2048], T.win[:, 0:1024], COPY), ["win0"], ["win1"])
+    op("s", lambda: S.activation(T.win[:, 2048:4096], T.win[:, 0:2048], COPY), ["win0", "win1"], ["win2"])
+    op("s", lambda: S.activation(T.win[:, 4096:5120], T.win[:, 0:1024], COPY), ["win0"], ["win3"])
+    select(T.E2[0:2, :], T.ONEF[0:2, :], [[1, 2], [0, 64]], A.is_equal, 0, ["ONEF"], ["E2"])
+    op("g", lambda: g.iota(T.J0[:], [[-8, 2], [-1, 2], [-2, 4]], 16, 1), (), ["J0"])
+    op("v", lambda: V.tensor_copy(T.LMF[0:2, 0:2], T.LM[0:2, 0:2]), ["LM"], ["LMF"])
+    mm(5, 0, 2, T.E2[0:2, :], T.LMF[0:2, 0:2], True, True, ["E2", "LMF"], "LH")
+    op("v", lambda: V.memset(T.Tab[:, 0:8], 0), (), ["TabZ"])
+    op("v", lambda: V.memset(T.Tab[:, 8200:8208], 0), (), ["TabY"])
+    op("v", lambda: V.memset(T.E[:, 0:1], 0.0), (), ["E0"])
+    for k in range(4):
+        op("v", lambda: V.memset(T.HM[:, 32 * k:32 * k + 32], -64.0 * (k % 2)), (), ["HM%d" % k])
+    op("v", lambda: V.tensor_scalar(T.B0[:, 0:256], T.A0[:], T.B5[:, 0:1], T.B5[:, 1:2], A.max, A.min),
+       ["A0", "LH"], ["clamp"], [0, 5])
+    op("v", lambda: V.tensor_tensor(T.FL[:], T.A0[:], T.B0[:, 0:256], A.is_equal), ["A0", "clamp"], ["FL"], [0])
+    for k in range(4):
+        op("s", lambda: S.activation(T.SC[:, 256 * k:256 * k + 256], T.FL[:], COPY, scale=0.0), ["FL"], ["SCz%d" % k])
+
+    mask = topo.mask(core, T.cores[peers[0]])
+
+    def send_all(src, dsts, sem, local):
+        g.remote_dma_fused([RemoteDMATransfer(dst_ids=[dst(r) for r in peers], dma_engine_mask=mask, remote_sem=T.sem[sem],
+                                              srcs=[src], dsts=dsts)], local_sem=T.sem[local])
+        total[local] = n_eng(peers[0])
+    deps("g", ["FL"])
+    send_all(T.FL[:], [T.fl[rank] for r in peers], "fl%d" % rank, "lf")
+    g.sem_inc(T.sem.gi, 1)
+    total["gi"] = 1
+
+    for b in range(2):
+        select(T["SH%d" % b][:], T.ONES[:], [[2, 8], [16, 16]], A.is_equal, b, ["ONES"], ["SH%d" % b])
+        select(T["SL%d" % b][:], T.ONES[:], [[2, 8], [16, 16]], A.is_equal, b - 128, ["ONES"], ["SL%d" % b])
+    select(T.PM[:], T.ONES[:], [[1, 8], [8, 16]], A.is_equal, 0, ["ONES"], ["PM"])
+    select(T.LT[:], T.ONES[:], [[1, 8], [8, 16]], A.is_gt, 0, ["ONES"], ["LT"])
+    op("g", lambda: g.iota(T.DD[:], [[16, 32]], 1024, 1, allow_small_or_imprecise_dtypes=True), (), ["DD"])
+    select(T.IDN[:], T.ONES[:], [[1, 128]], A.is_equal, 0, ["ONES"], ["IDN"])
+    for h in range(2):
+        for b in range(2):
+            n = "SE%d" % (2 * h + b)
+            select(T[n][:], T.ONES[:], [[2, 8], [32, 16]], A.is_equal, 16 * h + b, ["ONES"], [n])
+    for q in range(4):
+        n = "KH%d" % q
+        select(T[n][:], T.ONES[:, 0:64], [[0, 2], [64, 2], [1, 16]], A.is_equal, 16 * q, ["ONES"], [n])
+    op("g", lambda: g.iota(T.I5[:], [[0, 17], [1, 8]], 0, 0, allow_small_or_imprecise_dtypes=True), (), ["I5"])
+    select(T.SMA[:], T.ONEF[:, 0:32], [[1, 16], [16, 2]], A.is_equal, 0, ["ONEF"], ["SMA"])
+    for b in (32, 64, 96):
+        select(T.SMA[:], T.SMA[:], [[1, 16], [16, 2]], A.not_equal, b, ["SMA"], ["SMA"], 1.0)
+    select(T.PERM[:], T.ONEF[:], [[1, 16], [16, 8]], A.is_equal, 0, ["ONEF"], ["PERM"])
+
+    op("v", lambda: V.memset(T.win[:, 9216:16384], 0.0), (), ["win4"])
+    op("v", lambda: V.tensor_copy(T.FKU[:], T.FK[:]), ["FK"], ["FKU"])
+    op("v", lambda: V.tensor_scalar(T.J[:], T.J0[:], 15, None, A.bitwise_and), ["J0"], ["J"])
+    op("v", lambda: V.tensor_scalar(T.SELP[:], T.J[:], 0, None, A.is_equal), ["J"], ["SELP"])
+    op("v", lambda: V.tensor_scalar(T.HI[:], T.FK[:], 16256, None, A.bitwise_and), ["FK"], ["HI"])
+    op("v", lambda: V.tensor_scalar(T.LO[:], T.FK[:], 127, None, A.bitwise_and), ["FK"], ["LO"])
+    op("v", lambda: V.tensor_copy(T.HB[:], T.HI[:]), ["HI"], ["HB"])
+    op("v", lambda: V.tensor_scalar(T.LOB[:], T.LO[:], 8, None, A.add), ["LO"], ["LOB"])
+    op("s", lambda: S.activation(T.PMB[:], T.PM[:], COPY, scale=4096.0), ["PM"], ["PMB"])
+    for b in range(2):
+        c = 256 * b
+        mm(1, c, c + 256, T["SH%d" % b][:], T.HB[:], True, False, ["SH%d" % b, "HB"], "Xp")
+        mm(1, c, c + 256, T["SL%d" % b][:], T.LOB[:], False, True, ["SL%d" % b, "LOB"], "Xp")
+
+    need("y", [("gi", 1)])
+    fill(2)
+    fill(3)
+    for i in range(2):
+        table(i)
+    wins = ["win%d" % i for i in range(9)]
+    for r in [rank] + peers:
+        deps("y", wins)
+        src, name = (T.FL[:], "FL") if r == rank else (T.fl[r], "fl%d" % r)
+        dma("y", T.win[32 * r:32 * r + 32:16, :], src, "rl%d" % r, [name], ["wr%d" % r])
+    wr = ["wr%d" % r for r in range(4)]
+    for i in range(2, 16):
+        if i >= 7:
+            deps("y", ["Tab%d" % (i - 5)])
+        table(i)
+
+    chunks = [(0, 2), (8, 2), (2, 2), (10, 2), (4, 2), (12, 2), (6, 1), (14, 1), (7, 1), (15, 1)]
+    for u, n in chunks:
+        o, off = T.G[:, 256 * u:256 * (u + n)], T.FKU[:, 16 * u:16 * (u + n)]
+        if u < 8:
+            op("v", lambda: V.tensor_copy(o, T.win[:, 0:16384].indirect(off)), wr + wins + ["FKU"], ["Gf%d" % u])
+        else:
+            op("s", lambda: S.activation(o, T.win[:, 0:16384].indirect(off), COPY), wr + wins + ["FKU"], ["Gf%d" % u])
+    for u0, n in chunks:
+        for u in range(u0, u0 + n):
+            for b in range(2):
+                mm(0, 16 * b + u, 16 * b + u + 1, T.G[:, 256 * u + b:256 * u + 256:2], T.SELP[:, 0:1], True, True,
+                   ["Gf%d" % u0, "SELP"], "CNT")
+    op("v", lambda: V.tensor_copy(T.MB[:, 0:32], T.ME[:]), ["MEa", "MEb"], ["MB0"])
+    op("v", lambda: V.tensor_tensor(T.MR[:], T.ME[:], T.MB[:, 0:32], A.subtract), ["MEa", "MEb", "MB0"], ["MR"])
+    op("v", lambda: V.tensor_scalar(T.SV[:], T.B0[:, 0:32], 8, None, A.is_equal), ["CNT"], ["SV"], [0])
+    op("v", lambda: V.tensor_tensor_scan(T.E[:, 1:17], T.SV[:, 0:16], T.SV[:, 16:32], 0.0, A.add, A.add), ["SV"], ["E"])
+    op("v", lambda: V.tensor_copy(T.MB[:, 32:64], T.MR[:]), ["MR"], ["MB1"])
+    op("s", lambda: S.activation(T.X[:], T.B1[:], COPY), ["Xp"], ["X"], [1])
+    sv0, sv1, ee = T.SV[:, 0:16], T.SV[:, 16:32], T.E[:, 0:16]
+    mm(4, 0, 32, T.PMB[:], T.SV[:], True, True, ["PMB", "SV"], "SP")
+    mm(3, 0, 32, T.LT[:], T.SV[:], True, False, ["LT", "SV"], "WA")
+    mm(3, 0, 16, T.LT[:], sv1, False, False, ["LT", "SV"], "WA")
+    mm(3, 16, 32, T.LT[:], sv0, False, False, ["LT", "SV"], "WA")
+    mm(3, 16, 32, T.PM[:], sv0, False, False, ["PM", "SV"], "WA")
+    mm(3, 0, 16, T.ONES[:], ee, False, False, ["ONES", "E", "E0"], "WA")
+    mm(3, 16, 32, T.ONES[:], ee, False, True, ["ONES", "E", "E0"], "WA")
+    op("v", lambda: V.tensor_tensor(T.DN[:], T.DD[:], T.B4[:, 0:32], A.subtract), ["DD", "SP"], ["DN"], [4])
+    op("v", lambda: V.tensor_tensor(T.MB[:, 64:96], T.MR[:], T.MB[:, 32:64], A.subtract), ["MR", "MB1"], ["MB2"])
+    op("v", lambda: V.tensor_tensor(T.OFF[:], T.DN[:], T.B3[:, 0:32], A.max), ["DN", "WA"], ["OFF"], [3])
+    op("v", lambda: V.tensor_copy(T.POS[:], T.OFF[:]), ["OFF"], ["POS"])
+
+    op("v", lambda: V.tensor_copy(T.SC[:, 0:1664].indirect(T.POS[:]), T.X[:]), ["POS", "X"] + ["SCz%d" % k for k in range(4)],
+       ["SC"])
+    mm(6, 128, 256, T.MB[:], T.IDN[:], True, True, ["MB0", "MB1", "MB2", "IDN"], "MTp", 0, 96)
+    op("s", lambda: S.activation(T.MT[0:96, :], T.B6[0:96, 128:256], COPY), ["MTp"], ["MT"], [6])
+    mm(7, 0, 128, T.HM[:], T.ONES[:], True, False, ["HM%d" % k for k in range(4)] + ["ONES"], "KL")
+    for i in range(4):
+        h, b = i // 2, i % 2
+        c = 256 * b + 128 * h
+        mm(2, c, c + 128, T["SE%d" % i][0:96, :], T.MT[0:96, :], True, True, ["SE%d" % i, "MT"], "XMp")
+    op("s", lambda: S.activation(T.XM[:], T.B2[:], COPY), ["XMp"], ["XM"], [2])
+    for t in range(8):
+        mm(5, t, 128, T.SC[:, t:1024:8], T.SELP[:], True, True, ["SC", "SELP"], "KT", step=8)
+    op("v", lambda: V.tensor_copy(T.KB[:], T.B5[:, 0:128]), ["KT"], ["KB"], [5])
+    for q in range(4):
+        for e in range(2):
+            for p in range(2):
+                c = 64 * p + 32 * e
+                mm(7, 32 * q, 32 * q + 32, T["KH%d" % q][:], T.KB[:, c:c + 32], False, q == 3 and p == 1,
+                   ["KH%d" % q, "KB"], "KL", 64 * e, 64 * e + 64)
+    op("v", lambda: V.memset(T.SCM[:, 0:1024], 0.0), (), ["SCM"])
+    op("v", lambda: V.tensor_scalar(T.KS[:], T.B7[:, 0:128], 0, 8200, A.max, A.min), ["KL"], ["KS"], [7])
+    deps("g", ["KS"])
+    send_all(T.KS[:], [T["K%d" % rank][:] for r in peers], "kk%d" % rank, "lk")
+
+    op("v", lambda: V.tensor_copy(T.SCM[:, 0:1664].indirect(T.POS[:]), T.XM[:]), ["POS", "XM"], ["SCM"])
+    op("v", lambda: V.tensor_scalar(T.W0[:, 0:1], T.J[:, 0:1], 2, None, A.is_le), ["J"], ["W0"])
+    op("v", lambda: V.tensor_scalar(T.Z[:], T.I5[:], 7, T.W0[:, 0:1], A.is_equal, A.mult), ["I5", "W0"], ["Z"])
+    mm(4, 64, 65, T.ONES[:], T.E[:, 16:17], True, True, ["ONES", "E"], "CN")
+    for b in range(8):
+        mm(6, 0, 128, T.Z[:, 7 - b:135 - b], T.SCM[:, 128 * b:128 * b + 128], b == 0, b == 7, ["Z", "SCM"], "MEP")
+    op("v", lambda: V.memset(T.CT[:, 0:1], 0.0), (), ["CTz"])
+    op("v", lambda: V.tensor_copy(T.CT[:, 1:2], T.B4[:, 64:65]), ["CN"], ["CT"], [4])
+    dma("y", T.y[:, 1023:1025], T.CT[0:16, :], "d_ct", ["CT", "CTz"], ["yct"])
+
+    tabs = ["TabZ", "TabY"] + ["Tab%d" % i for i in range(16)]
+    es_bank = {rank: 3, peers[0]: 4, peers[1]: 7, peers[2]: 5}
+
+    def pick(r, q):
+        lst, name = (T.KS, "KS") if r == rank else (T["K%d" % r], "K%d" % r)
+        off = lst[:, 32 * q + 8 * rank:32 * q + 8 * rank + 8]
+        o = T["G%d" % r][:, 128 * q:128 * q + 128]
+        if q < 2:
+            op("v", lambda: V.tensor_copy(o, T.Tab[:, 0:8208].indirect(off)), tabs + [name], ["GA%d%d" % (r, q)])
+        else:
+            op("s", lambda: S.activation(o, T.Tab[:, 0:8208].indirect(off), COPY), tabs + [name], ["GA%d%d" % (r, q)])
+
+    def add(r):
+        for q in (0, 2, 1, 3):
+            mm(es_bank[r], 128 + q, 256, T["G%d" % r][:, 128 * q:128 * q + 128], T.SMA[:], True, True,
+               ["SMA", "GA%d%d" % (r, q)], "ES%d" % r, step=4)
+
+    def sums(r, e):
+        o = T["B%d" % es_bank[r]][:, 128:256]
+        if e == "v":
+            op("v", lambda: V.tensor_copy(T["R%d" % r][:], o), ["ES%d" % r], ["RS%d" % r], [es_bank[r]])
+        else:
+            op("s", lambda: S.activation(T["R%d" % r][:], o, COPY), ["ES%d" % r], ["RS%d" % r], [es_bank[r]])
+
+    p0, p1, p2 = peers
+    for r in peers + [rank]:
+        pick(r, 0)
+        pick(r, 1)
+    for r in (p0, p1):
+        pick(r, 2)
+        pick(r, 3)
+        add(r)
+    sums(p0, "s")
+    pick(p2, 2)
+    pick(p2, 3)
+    add(p2)
+    pick(rank, 2)
+    pick(rank, 3)
+    sums(p1, "v")
+    sums(p2, "s")
+    op("v", lambda: V.tensor_copy(T.M1[:], T.B6[:, 0:128]), ["MEP"], ["M1"], [6])
+    add(rank)
+    for r in peers:
+        deps("g", ["RS%d" % r])
+        rid, pid, _ = topo.addr(T.cores[r])
+        g.remote_dma(T["P%d" % rank][:], T["R%d" % r][:], T.sem["ps%d" % rank], T.sem.lp, pid, rid, topo.mask(core, T.cores[r]))
+        total["lp"] = total.get("lp", 0) + n_eng(r)
+
+    own = T["B%d" % es_bank[rank]][:, 128:256]
+    op("v", lambda: V.tensor_tensor(T.B0[:, 256:384], T["P%d" % p0][:], own, A.add), ["P%d" % p0, "ES%d" % rank], ["Q0"],
+       [0, es_bank[rank]])
+    op("v", lambda: V.tensor_tensor(T["R%d" % rank][:], T["P%d" % p1][:], T.B0[:, 256:384], A.add), ["P%d" % p1, "Q0"],
+       ["Q1"], [0])
+    mm(2, 0, 128, T["R%d" % rank][:], T.PERM[:], True, False, ["Q1", "PERM"], "SUM")
+    mm(2, 0, 128, T["P%d" % p2][:], T.PERM[:], False, True, ["P%d" % p2, "PERM"], "SUM")
+    op("v", lambda: V.tensor_tensor(T.YF[:], T.M1[:], T.B2[:, 0:128], A.add), ["M1", "SUM"], ["F"], [2])
+    deps("y", ["yct"])
+    dma("y", T.y[:, 0:1024], T.YF[:], "d_y", ["F"], ["y"])
+    need("g", list(total.items()))

@@ -1,20 +1,23 @@
 from concourse.bass import DstId, RemoteDMATransfer
 from concourse.mybir import AluOpType, ActivationFunctionType
 
+FILL_S, FILL_D = 4608, 3
+EARLY = 1
+SPARE = 6144
 SCRATCH = {"fl": ("dram", [4, 128, 256], "bfloat16")}
 for _t, _l in {
-    "int32": "A0:256 LM:4 FK:256 HI:256 LO:256 ME:32 MR:32 J0:16 J:16 Tab:8208 OFF:32",
-    "uint16": "FKU:256 POS:32 KS:128 K0:128 K1:128 K2:128 K3:128",
-    "bfloat16": "FL:256 G:4096 HB:256 LOB:256 X:512 MB:96 MT:128 XM:512 SC:1664 SCM:1664 SELP:16 ONES:128 LT:128 KB:128 "
-                "PM:128 PMB:128 IDN:128 KH0:64 KH1:64 KH2:64 KH3:64 HM:128 SH0:128 SH1:128 SL0:128 SL1:128 "
-                "SE0:128 SE1:128 SE2:128 SE3:128 Z:136 SV:32 E:32 win:16384",
-    "float32": "LMF:4 E2:128 ONEF:128 I5:136 DD:32 SMA:32 PERM:128 W0:8 DN:32 "
-               "G0:512 G1:512 G2:512 G3:512 P0:128 P1:128 P2:128 P3:128 R0:128 R1:128 R2:128 R3:128 M1:128 CT:2 YF:128",
+    "int32": "A0:256 LM:4 FK:256 ME:32 MR:32 J0:16 J:16 Tab:8208",
+    "uint16": "FKU:256 POS:32 KS:128 K0:32 K1:32 K2:32 K3:32",
+    "bfloat16": "FL:256 G:4096 HB:256 LOB:256 X:512 MB:96 MT:128 XM:512 SC:%d SCM:%d SELP:16 SELB:2 ONES:144 LT:128 KB:128 "
+                "LE:128 IDN:128 KH0:64 KH1:64 KH2:64 KH3:64 HM:128 SH:264 "
+                "SE0:128 SE1:128 SE2:128 SE3:128 Z:136 SV:32 E:32 win:16384" % (SPARE, SPARE),
+    "float32": "LMF:4 E2:128 ONEF:128 DD:32 SMA:32 PERM:128 PM:128 NS:32 "
+               "G0:512 G1:512 G2:512 G3:512 P0:128 P1:128 P2:128 P3:128 R0:128 R1:128 R2:128 R3:128 CT:2 YF:128",
 }.items():
     for _x in _l.split():
         SCRATCH[_x.split(":")[0]] = ("sbuf", [128, int(_x.split(":")[1])], _t)
 for _b in range(8):
-    SCRATCH["B%d" % _b] = ("psum", [128, 512], "float32")
+    SCRATCH["B%d" % _b] = ("psum", [128, 16, 4, 8] if _b == 7 else [128, 512], "float32")
 SEMAPHORES = (["q_v", "q_s", "q_t", "q_g", "lf", "lk", "lp", "gi"]
               + ["%s%d" % (a, i) for a in ("fl", "kk", "ps", "rl", "dz") for i in range(4)]
               + ["d_" + n for n in ("lim", "at0", "fk", "me", "ct", "y")] + ["tb%d" % i for i in range(16)])
@@ -84,7 +87,7 @@ def rank_program(g, core, T, topo):
         total[sem] = n
 
     peers = [r for r in range(4) if r != rank]
-    peers.sort(key=lambda r: not topo.same_plane(topo.chip(core), topo.chip(T.cores[r])))
+    peers.sort(key=lambda r: (not topo.same_plane(topo.chip(core), topo.chip(T.cores[r])), r ^ rank))
 
     def n_eng(r):
         return len(topo.engines(core, T.cores[r]))
@@ -104,10 +107,13 @@ def rank_program(g, core, T, topo):
     def mm(bank, c0, c1, lhs, rhs, a, z, reads, name, p0=0, p1=128, step=1):
         op("t", lambda: P.matmul(T["B%d" % bank][p0:p1, c0:c1:step], lhs, rhs, a, z), reads, [name], [bank], join=True)
 
-    def select(out, in_, pattern, how, base, reads, writes, fill=0.0):
-        op("g", lambda: g.affine_select(out, in_, pattern, how, fill, base, -1), reads, writes)
+    def select(out, in_, pattern, how, base, reads, writes, fill=0.0, step=-1):
+        op("g", lambda: g.affine_select(out, in_, pattern, how, fill, base, step), reads, writes)
 
-    dma("y", T.LM[0:2, 0:2], T.lim[:], "d_lim", (), ["LM"])
+    def ramp(out, pattern, base, step, name):
+        op("g", lambda: g.iota(out, pattern, base, step, allow_small_or_imprecise_dtypes=True), (), [name])
+
+    dma("s", T.LM[0:2, 0:2], T.lim[:], "d_lim", (), ["LM"])
     dma("y", T.A0[:], T.at[0:1, :], "d_at0", (), ["A0"])
     dma("y", T.FK[:], T.fk[:], "d_fk", (), ["FK"])
     dma("y", T.ME[:, 0:16], T.me[0:1, 0:2048], "d_me", (), ["MEa"])
@@ -118,32 +124,28 @@ def rank_program(g, core, T, topo):
         p, s = 64 * e + 32 * h + 16 * x, 16384 * e + 8192 * h + c
         dma("y", T.Tab[p:p + 16, 8 + c:8 + c + 4096], T.at[:, s:s + 4096], "tb%d" % i, (), ["Tab%d" % i])
 
-    def fill(k):
-        c = 5120 + 1024 * k
-        dma("y", T.win[:, c:c + 1024], T.win[:, 0:1024], "dz%d" % k, ["win0"], ["win%d" % (5 + k)])
-
+    cs, cv = 1024 + FILL_S, 1024 + FILL_S + 1024 * FILL_D
+    ones = T.ONES[:, 0:128]
     op("v", lambda: V.memset(T.ONEF[:], 1.0), (), ["ONEF"])
     op("v", lambda: V.memset(T.win[:, 0:1024], 0.0), (), ["win0"])
-    op("v", lambda: V.memset(T.ONES[:], 1.0), (), ["ONES"])
-    fill(0)
-    fill(1)
+    for k in range(FILL_D):
+        c = cs + 1024 * k
+        dma("y", T.win[:, c:c + 1024], T.win[:, 0:1024], "dz%d" % k, ["win0"], ["win%d" % (5 + k)])
     op("s", lambda: S.activation(T.win[:, 1024:2048], T.win[:, 0:1024], COPY), ["win0"], ["win1"])
     op("s", lambda: S.activation(T.win[:, 2048:4096], T.win[:, 0:2048], COPY), ["win0", "win1"], ["win2"])
-    op("s", lambda: S.activation(T.win[:, 4096:5120], T.win[:, 0:1024], COPY), ["win0"], ["win3"])
+    op("s", lambda: S.activation(T.win[:, 4096:cs], T.win[:, 0:cs - 4096], COPY), ["win0", "win1"], ["win3"])
     select(T.E2[0:2, :], T.ONEF[0:2, :], [[1, 2], [0, 64]], A.is_equal, 0, ["ONEF"], ["E2"])
     op("g", lambda: g.iota(T.J0[:], [[-8, 2], [-1, 2], [-2, 4]], 16, 1), (), ["J0"])
+    op("g", lambda: g.iota(T.Tab[:, 0:8], [[0, 8]], 0, 0), (), ["TabZ"])
+    op("g", lambda: g.iota(T.Tab[:, 8200:8208], [[0, 8]], 0, 0), (), ["TabY"])
+    ramp(T.E[:, 0:1], [[0, 1]], 0, 0, "E0")
+    ramp(T.SH[:, 0:8], [[0, 8]], 0, 0, "SHz")
     op("v", lambda: V.tensor_copy(T.LMF[0:2, 0:2], T.LM[0:2, 0:2]), ["LM"], ["LMF"])
     mm(5, 0, 2, T.E2[0:2, :], T.LMF[0:2, 0:2], True, True, ["E2", "LMF"], "LH")
-    op("v", lambda: V.memset(T.Tab[:, 0:8], 0), (), ["TabZ"])
-    op("v", lambda: V.memset(T.Tab[:, 8200:8208], 0), (), ["TabY"])
-    op("v", lambda: V.memset(T.E[:, 0:1], 0.0), (), ["E0"])
-    for k in range(4):
-        op("v", lambda: V.memset(T.HM[:, 32 * k:32 * k + 32], -64.0 * (k % 2)), (), ["HM%d" % k])
+    op("v", lambda: V.memset(T.ONES[:], 1.0), (), ["ONES"])
     op("v", lambda: V.tensor_scalar(T.B0[:, 0:256], T.A0[:], T.B5[:, 0:1], T.B5[:, 1:2], A.max, A.min),
        ["A0", "LH"], ["clamp"], [0, 5])
-    op("v", lambda: V.tensor_tensor(T.FL[:], T.A0[:], T.B0[:, 0:256], A.is_equal), ["A0", "clamp"], ["FL"], [0])
-    for k in range(4):
-        op("s", lambda: S.activation(T.SC[:, 256 * k:256 * k + 256], T.FL[:], COPY, scale=0.0), ["FL"], ["SCz%d" % k])
+    op("v", lambda: V.tensor_tensor(T.FL[:], T.A0[:], T.B0[:, 0:256], A.not_equal), ["A0", "clamp"], ["FL"], [0])
 
     mask = topo.mask(core, T.cores[peers[0]])
 
@@ -157,52 +159,52 @@ def rank_program(g, core, T, topo):
     total["gi"] = 1
 
     for b in range(2):
-        select(T["SH%d" % b][:], T.ONES[:], [[2, 8], [16, 16]], A.is_equal, b, ["ONES"], ["SH%d" % b])
-        select(T["SL%d" % b][:], T.ONES[:], [[2, 8], [16, 16]], A.is_equal, b - 128, ["ONES"], ["SL%d" % b])
-    select(T.PM[:], T.ONES[:], [[1, 8], [8, 16]], A.is_equal, 0, ["ONES"], ["PM"])
-    select(T.LT[:], T.ONES[:], [[1, 8], [8, 16]], A.is_gt, 0, ["ONES"], ["LT"])
-    op("g", lambda: g.iota(T.DD[:], [[16, 32]], 1024, 1, allow_small_or_imprecise_dtypes=True), (), ["DD"])
-    select(T.IDN[:], T.ONES[:], [[1, 128]], A.is_equal, 0, ["ONES"], ["IDN"])
+        select(T.SH[:, 8 + 128 * b:136 + 128 * b], ones, [[2, 8], [16, 16]], A.is_equal, b, ["ONES"], ["SH%d" % b])
+    select(T.LT[:], ones, [[1, 8], [8, 16]], A.is_gt, 0, ["ONES"], ["LT"])
+    select(T.LE[:], ones, [[1, 8], [8, 16]], A.is_ge, 0, ["ONES"], ["LE"])
+    select(T.PM[:], T.ONEF[:], [[1, 8], [8, 16]], A.is_equal, 0, ["ONEF"], ["PM"])
+    ramp(T.DD[:], [[1, 2], [256, 16]], 1024, 2, "DD")
+    ramp(T.SC[:, 0:1024], [[0, 1024]], 0, 0, "SC")
+    select(T.IDN[:], ones, [[1, 128]], A.is_equal, 0, ["ONES"], ["IDN"])
+    ramp(T.HM[:], [[0, 2], [-64, 2], [0, 32]], 0, 0, "HM")
+    ramp(T.CT[:, 0:1], [[0, 1]], 0, 0, "CTz")
     for h in range(2):
         for b in range(2):
             n = "SE%d" % (2 * h + b)
-            select(T[n][:], T.ONES[:], [[2, 8], [32, 16]], A.is_equal, 16 * h + b, ["ONES"], [n])
+            select(T[n][:], ones, [[2, 8], [32, 16]], A.is_equal, 16 * h + b, ["ONES"], [n])
     for q in range(4):
         n = "KH%d" % q
         select(T[n][:], T.ONES[:, 0:64], [[0, 2], [64, 2], [1, 16]], A.is_equal, 16 * q, ["ONES"], [n])
-    op("g", lambda: g.iota(T.I5[:], [[0, 17], [1, 8]], 0, 0, allow_small_or_imprecise_dtypes=True), (), ["I5"])
     select(T.SMA[:], T.ONEF[:, 0:32], [[1, 16], [16, 2]], A.is_equal, 0, ["ONEF"], ["SMA"])
     for b in (32, 64, 96):
         select(T.SMA[:], T.SMA[:], [[1, 16], [16, 2]], A.not_equal, b, ["SMA"], ["SMA"], 1.0)
     select(T.PERM[:], T.ONEF[:], [[1, 16], [16, 8]], A.is_equal, 0, ["ONEF"], ["PERM"])
+    select(T.Z[:], T.ONES[:, 0:136], [[0, 17], [1, 8]], A.is_equal, -7, ["ONES"], ["Z"], step=0)
 
-    op("v", lambda: V.memset(T.win[:, 9216:16384], 0.0), (), ["win4"])
+    op("v", lambda: V.memset(T.win[:, cv:16384], 0.0), (), ["win4"])
+    op("v", lambda: V.tensor_scalar(T.B6[:, 0:256], T.FK[:], 8, None, A.add), ["FK"], ["K8"], [6])
+    op("s", lambda: S.activation(T.HB[:], T.B6[:, 0:256], COPY), ["K8"], ["HB"], [6])
     op("v", lambda: V.tensor_copy(T.FKU[:], T.FK[:]), ["FK"], ["FKU"])
     op("v", lambda: V.tensor_scalar(T.J[:], T.J0[:], 15, None, A.bitwise_and), ["J0"], ["J"])
+    op("v", lambda: V.tensor_tensor(T.LOB[:], T.B6[:, 0:256], T.HB[:], A.subtract), ["K8", "HB"], ["LOB"], [6])
+    op("v", lambda: V.tensor_scalar(T.SELB[:, 0:1], T.J[:, 0:1], 0, 8192, A.is_equal, A.mult), ["J"], ["SELB"])
     op("v", lambda: V.tensor_scalar(T.SELP[:], T.J[:], 0, None, A.is_equal), ["J"], ["SELP"])
-    op("v", lambda: V.tensor_scalar(T.HI[:], T.FK[:], 16256, None, A.bitwise_and), ["FK"], ["HI"])
-    op("v", lambda: V.tensor_scalar(T.LO[:], T.FK[:], 127, None, A.bitwise_and), ["FK"], ["LO"])
-    op("v", lambda: V.tensor_copy(T.HB[:], T.HI[:]), ["HI"], ["HB"])
-    op("v", lambda: V.tensor_scalar(T.LOB[:], T.LO[:], 8, None, A.add), ["LO"], ["LOB"])
-    op("s", lambda: S.activation(T.PMB[:], T.PM[:], COPY, scale=4096.0), ["PM"], ["PMB"])
     for b in range(2):
-        c = 256 * b
-        mm(1, c, c + 256, T["SH%d" % b][:], T.HB[:], True, False, ["SH%d" % b, "HB"], "Xp")
-        mm(1, c, c + 256, T["SL%d" % b][:], T.LOB[:], False, True, ["SL%d" % b, "LOB"], "Xp")
+        c, n = 256 * b, ["SHz", "SH0", "SH1"]
+        mm(1, c, c + 256, T.SH[:, 8 + 128 * b:136 + 128 * b], T.HB[:], True, False, n + ["HB"], "Xp")
+        mm(1, c, c + 256, T.SH[:, 128 * b:128 + 128 * b], T.LOB[:], False, True, n + ["LOB"], "Xp")
 
     need("y", [("gi", 1)])
-    fill(2)
-    fill(3)
-    for i in range(2):
+    for i in range(EARLY):
         table(i)
-    wins = ["win%d" % i for i in range(9)]
+    wins = ["win%d" % i for i in range(5 + FILL_D)]
     for r in [rank] + peers:
         deps("y", wins)
         src, name = (T.FL[:], "FL") if r == rank else (T.fl[r], "fl%d" % r)
         dma("y", T.win[32 * r:32 * r + 32:16, :], src, "rl%d" % r, [name], ["wr%d" % r])
     wr = ["wr%d" % r for r in range(4)]
-    for i in range(2, 16):
-        if i >= 7:
+    for i in range(EARLY, 16):
+        if i >= EARLY + 5:
             deps("y", ["Tab%d" % (i - 5)])
         table(i)
 
@@ -216,37 +218,37 @@ def rank_program(g, core, T, topo):
     for u0, n in chunks:
         for u in range(u0, u0 + n):
             for b in range(2):
-                mm(0, 16 * b + u, 16 * b + u + 1, T.G[:, 256 * u + b:256 * u + 256:2], T.SELP[:, 0:1], True, True,
-                   ["Gf%d" % u0, "SELP"], "CNT")
+                mm(0, 16 * b + u, 16 * b + u + 1, T.G[:, 256 * u + b:256 * u + 256:2], T.SELB[:, 0:1], True, True,
+                   ["Gf%d" % u0, "SELB"], "CNT")
     op("v", lambda: V.tensor_copy(T.MB[:, 0:32], T.ME[:]), ["MEa", "MEb"], ["MB0"])
-    op("v", lambda: V.tensor_tensor(T.MR[:], T.ME[:], T.MB[:, 0:32], A.subtract), ["MEa", "MEb", "MB0"], ["MR"])
-    op("v", lambda: V.tensor_scalar(T.SV[:], T.B0[:, 0:32], 8, None, A.is_equal), ["CNT"], ["SV"], [0])
+    op("v", lambda: V.tensor_scalar(T.SV[:], T.B0[:, 0:32], 0, None, A.is_equal), ["CNT"], ["SV"], [0])
+    op("v", lambda: V.tensor_tensor(T.NS[:], T.B0[:, 0:32], T.DD[:], A.min), ["CNT", "DD"], ["NS"], [0])
     op("v", lambda: V.tensor_tensor_scan(T.E[:, 1:17], T.SV[:, 0:16], T.SV[:, 16:32], 0.0, A.add, A.add), ["SV"], ["E"])
-    op("v", lambda: V.tensor_copy(T.MB[:, 32:64], T.MR[:]), ["MR"], ["MB1"])
+    op("v", lambda: V.tensor_tensor(T.MR[:], T.ME[:], T.MB[:, 0:32], A.subtract), ["MEa", "MEb", "MB0"], ["MR"])
     op("s", lambda: S.activation(T.X[:], T.B1[:], COPY), ["Xp"], ["X"], [1])
     sv0, sv1, ee = T.SV[:, 0:16], T.SV[:, 16:32], T.E[:, 0:16]
-    mm(4, 0, 32, T.PMB[:], T.SV[:], True, True, ["PMB", "SV"], "SP")
     mm(3, 0, 32, T.LT[:], T.SV[:], True, False, ["LT", "SV"], "WA")
     mm(3, 0, 16, T.LT[:], sv1, False, False, ["LT", "SV"], "WA")
-    mm(3, 16, 32, T.LT[:], sv0, False, False, ["LT", "SV"], "WA")
-    mm(3, 16, 32, T.PM[:], sv0, False, False, ["PM", "SV"], "WA")
-    mm(3, 0, 16, T.ONES[:], ee, False, False, ["ONES", "E", "E0"], "WA")
-    mm(3, 16, 32, T.ONES[:], ee, False, True, ["ONES", "E", "E0"], "WA")
-    op("v", lambda: V.tensor_tensor(T.DN[:], T.DD[:], T.B4[:, 0:32], A.subtract), ["DD", "SP"], ["DN"], [4])
+    mm(3, 16, 32, T.LE[:], sv0, False, False, ["LE", "SV"], "WA")
+    mm(3, 0, 32, T.PM[:], T.NS[:], False, False, ["PM", "NS"], "WA")
+    mm(3, 0, 16, ones, ee, False, False, ["ONES", "E", "E0"], "WA")
+    mm(3, 16, 32, ones, ee, False, True, ["ONES", "E", "E0"], "WA")
+    op("v", lambda: V.tensor_copy(T.MB[:, 32:64], T.MR[:]), ["MR"], ["MB1"])
+    op("v", lambda: V.tensor_copy(T.POS[:], T.B3[:, 0:32]), ["WA"], ["POS"], [3])
     op("v", lambda: V.tensor_tensor(T.MB[:, 64:96], T.MR[:], T.MB[:, 32:64], A.subtract), ["MR", "MB1"], ["MB2"])
-    op("v", lambda: V.tensor_tensor(T.OFF[:], T.DN[:], T.B3[:, 0:32], A.max), ["DN", "WA"], ["OFF"], [3])
-    op("v", lambda: V.tensor_copy(T.POS[:], T.OFF[:]), ["OFF"], ["POS"])
 
-    op("v", lambda: V.tensor_copy(T.SC[:, 0:1664].indirect(T.POS[:]), T.X[:]), ["POS", "X"] + ["SCz%d" % k for k in range(4)],
-       ["SC"])
+    op("v", lambda: V.tensor_copy(T.SC[:].indirect(T.POS[:]), T.X[:]), ["POS", "X"], ["SC"])
+    mm(4, 64, 65, ones, T.E[:, 16:17], True, True, ["ONES", "E"], "CN")
     mm(6, 128, 256, T.MB[:], T.IDN[:], True, True, ["MB0", "MB1", "MB2", "IDN"], "MTp", 0, 96)
     op("s", lambda: S.activation(T.MT[0:96, :], T.B6[0:96, 128:256], COPY), ["MTp"], ["MT"], [6])
-    mm(7, 0, 128, T.HM[:], T.ONES[:], True, False, ["HM%d" % k for k in range(4)] + ["ONES"], "KL")
+    op("t", lambda: P.matmul(T.B7[:, 0:4], T.HM[:], ones, True, False), ["HM", "ONES"], ["KL"], [7], join=True)
     for i in range(4):
         h, b = i // 2, i % 2
         c = 256 * b + 128 * h
         mm(2, c, c + 128, T["SE%d" % i][0:96, :], T.MT[0:96, :], True, True, ["SE%d" % i, "MT"], "XMp")
     op("s", lambda: S.activation(T.XM[:], T.B2[:], COPY), ["XMp"], ["XM"], [2])
+    op("s", lambda: S.activation(T.CT[:, 1:2], T.B4[:, 64:65], COPY), ["CN"], ["CT"], [4])
+    dma("y", T.y[:, 1023:1025], T.CT[0:16, :], "d_ct", ["CT", "CTz"], ["yct"])
     for t in range(8):
         mm(5, t, 128, T.SC[:, t:1024:8], T.SELP[:], True, True, ["SC", "SELP"], "KT", step=8)
     op("v", lambda: V.tensor_copy(T.KB[:], T.B5[:, 0:128]), ["KT"], ["KB"], [5])
@@ -254,29 +256,31 @@ def rank_program(g, core, T, topo):
         for e in range(2):
             for p in range(2):
                 c = 64 * p + 32 * e
-                mm(7, 32 * q, 32 * q + 32, T["KH%d" % q][:], T.KB[:, c:c + 32], False, q == 3 and p == 1,
-                   ["KH%d" % q, "KB"], "KL", 64 * e, 64 * e + 64)
+                op("t", lambda: P.matmul(T.B7[64 * e:64 * e + 64, q], T["KH%d" % q][:], T.KB[:, c:c + 32], False, q == 3 and p == 1),
+                   ["KH%d" % q, "KB"], ["KL"], [7], join=True)
     op("v", lambda: V.memset(T.SCM[:, 0:1024], 0.0), (), ["SCM"])
-    op("v", lambda: V.tensor_scalar(T.KS[:], T.B7[:, 0:128], 0, 8200, A.max, A.min), ["KL"], ["KS"], [7])
-    deps("g", ["KS"])
-    send_all(T.KS[:], [T["K%d" % rank][:] for r in peers], "kk%d" % rank, "lk")
 
-    op("v", lambda: V.tensor_copy(T.SCM[:, 0:1664].indirect(T.POS[:]), T.XM[:]), ["POS", "XM"], ["SCM"])
-    op("v", lambda: V.tensor_scalar(T.W0[:, 0:1], T.J[:, 0:1], 2, None, A.is_le), ["J"], ["W0"])
-    op("v", lambda: V.tensor_scalar(T.Z[:], T.I5[:], 7, T.W0[:, 0:1], A.is_equal, A.mult), ["I5", "W0"], ["Z"])
-    mm(4, 64, 65, T.ONES[:], T.E[:, 16:17], True, True, ["ONES", "E"], "CN")
-    for b in range(8):
-        mm(6, 0, 128, T.Z[:, 7 - b:135 - b], T.SCM[:, 128 * b:128 * b + 128], b == 0, b == 7, ["Z", "SCM"], "MEP")
-    op("v", lambda: V.memset(T.CT[:, 0:1], 0.0), (), ["CTz"])
-    op("v", lambda: V.tensor_copy(T.CT[:, 1:2], T.B4[:, 64:65]), ["CN"], ["CT"], [4])
-    dma("y", T.y[:, 1023:1025], T.CT[0:16, :], "d_ct", ["CT", "CTz"], ["yct"])
+    def send(r, out, in_, sem, local):
+        rid, pid, _ = topo.addr(T.cores[r])
+        g.remote_dma(out, in_, T.sem[sem], T.sem[local], pid, rid, topo.mask(core, T.cores[r]))
+        total[local] = total.get(local, 0) + n_eng(r)
+    for r in peers + [rank]:
+        op("v", lambda: V.tensor_scalar(T.KS[:, 32 * r:32 * r + 32], T.B7[:, 0:4, r, :], 0, 8200, A.max, A.min), ["KL"], ["KS%d" % r], [7])
+        if r != rank:
+            deps("g", ["KS%d" % r])
+            send(r, T["K%d" % rank][:], T.KS[:, 32 * r:32 * r + 32], "kk%d" % rank, "lk")
+
+    def measures(b):
+        op("v", lambda: V.tensor_copy(T.SCM[:].indirect(T.POS[:, 16 * b:16 * b + 16]), T.XM[:, 256 * b:256 * b + 256]),
+           ["POS", "XM"], ["SCM"])
+    measures(0)
 
     tabs = ["TabZ", "TabY"] + ["Tab%d" % i for i in range(16)]
-    es_bank = {rank: 3, peers[0]: 4, peers[1]: 7, peers[2]: 5}
+    es_bank = {rank: 3, peers[0]: 4, peers[1]: 1, peers[2]: 5}
 
     def pick(r, q):
-        lst, name = (T.KS, "KS") if r == rank else (T["K%d" % r], "K%d" % r)
-        off = lst[:, 32 * q + 8 * rank:32 * q + 8 * rank + 8]
+        lst, name, c = (T.KS, "KS%d" % r, 32 * r) if r == rank else (T["K%d" % r], "K%d" % r, 0)
+        off = lst[:, c + 8 * q:c + 8 * q + 8]
         o = T["G%d" % r][:, 128 * q:128 * q + 128]
         if q < 2:
             op("v", lambda: V.tensor_copy(o, T.Tab[:, 0:8208].indirect(off)), tabs + [name], ["GA%d%d" % (r, q)])
@@ -307,26 +311,26 @@ def rank_program(g, core, T, topo):
     pick(p2, 2)
     pick(p2, 3)
     add(p2)
+    sums(p1, "s")
     pick(rank, 2)
     pick(rank, 3)
-    sums(p1, "v")
     sums(p2, "s")
-    op("v", lambda: V.tensor_copy(T.M1[:], T.B6[:, 0:128]), ["MEP"], ["M1"], [6])
     add(rank)
+    measures(1)
     for r in peers:
         deps("g", ["RS%d" % r])
-        rid, pid, _ = topo.addr(T.cores[r])
-        g.remote_dma(T["P%d" % rank][:], T["R%d" % r][:], T.sem["ps%d" % rank], T.sem.lp, pid, rid, topo.mask(core, T.cores[r]))
-        total["lp"] = total.get("lp", 0) + n_eng(r)
+        send(r, T["P%d" % rank][:], T["R%d" % r][:], "ps%d" % rank, "lp")
 
+    for b in range(8):
+        mm(2, 0, 128, T.Z[:, 7 - b:135 - b], T.SCM[:, 128 * b:128 * b + 128], b == 0, False, ["Z", "SCM"], "SUM")
     own = T["B%d" % es_bank[rank]][:, 128:256]
     op("v", lambda: V.tensor_tensor(T.B0[:, 256:384], T["P%d" % p0][:], own, A.add), ["P%d" % p0, "ES%d" % rank], ["Q0"],
        [0, es_bank[rank]])
     op("v", lambda: V.tensor_tensor(T["R%d" % rank][:], T["P%d" % p1][:], T.B0[:, 256:384], A.add), ["P%d" % p1, "Q0"],
        ["Q1"], [0])
-    mm(2, 0, 128, T["R%d" % rank][:], T.PERM[:], True, False, ["Q1", "PERM"], "SUM")
+    mm(2, 0, 128, T["R%d" % rank][:], T.PERM[:], False, False, ["Q1", "PERM"], "SUM")
     mm(2, 0, 128, T["P%d" % p2][:], T.PERM[:], False, True, ["P%d" % p2, "PERM"], "SUM")
-    op("v", lambda: V.tensor_tensor(T.YF[:], T.M1[:], T.B2[:, 0:128], A.add), ["M1", "SUM"], ["F"], [2])
+    op("v", lambda: V.tensor_copy(T.YF[:], T.B2[:, 0:128]), ["SUM"], ["F"], [2])
     deps("y", ["yct"])
     dma("y", T.y[:, 0:1024], T.YF[:], "d_y", ["F"], ["y"])
     need("g", list(total.items()))

from concourse.bass import DstId, RemoteDMATransfer
from concourse.mybir import AluOpType, ActivationFunctionType

FILL_S, FILL_D = 4608, 3
EARLY = 1
SPARE = 6144
SCRATCH = {"fl": ("dram", [4, 128, 256], "bfloat16")}
for _t, _l in {
    "int32": "A0:256 LM:4 FK:256 ME:32 MR:32 J0:16 J:16 Tab:8208",
    "uint16": "FKU:256 POS:32 KS:128 K0:32 K1:32 K2:32 K3:32",
    "bfloat16": "FL:256 G:4096 HB:256 LOB:256 X:512 MB:96 MT:128 XM:512 SC:%d SCM:%d SELP:16 SELB:2 ONES:144 LT:128 KB:128 "
                "LE:128 IDN:128 KH0:64 KH1:64 KH2:64 KH3:64 HM:128 SH:264 "
                "SE0:128 SE1:128 SE2:128 SE3:128 Z:136 SV:32 E:32 win:16384" % (SPARE, SPARE),
    "float32": "LMF:4 E2:128 ONEF:128 DD:32 SMA:32 PERM:128 PM:128 NS:32 "
               "G0:512 G1:512 G2:512 G3:512 P0:128 P1:128 P2:128 P3:128 R0:128 R1:128 R2:128 R3:128 CT:2 YF:128",
}.items():
    for _x in _l.split():
        SCRATCH[_x.split(":")[0]] = ("sbuf", [128, int(_x.split(":")[1])], _t)
for _b in range(8):
    SCRATCH["B%d" % _b] = ("psum", [128, 16, 4, 8] if _b == 7 else [128, 512], "float32")
SEMAPHORES = (["q_v", "q_s", "q_t", "q_g", "lf", "lk", "lp", "gi"]
              + ["%s%d" % (a, i) for a in ("fl", "kk", "ps", "rl", "dz") for i in range(4)]
              + ["d_" + n for n in ("lim", "at0", "fk", "me", "ct", "y")] + ["tb%d" % i for i in range(16)])


def rank_program(g, core, T, topo):
    rank = T.rank_of(core)
    if rank is None:
        return
    A = AluOpType
    COPY = ActivationFunctionType.Copy
    eng = {"v": g.vector, "s": g.scalar, "t": g.tensor, "g": g, "y": g.sync}
    seen = {e: {} for e in eng}
    total = {}
    know = {}
    lastw, reads_of, bank_of = {}, {}, {}

    def need(e, toks):
        for s, v in sorted(toks):
            if seen[e].get(s, 0) < v:
                eng[e].wait_ge(T.sem[s], v)
                for s2, v2 in know.get((s, v), {}).items():
                    seen[e][s2] = max(seen[e].get(s2, 0), v2)
                seen[e][s] = max(seen[e].get(s, 0), v)

    def deps(e, reads, writes=(), banks=()):
        d = {}

        def put(tok):
            d[tok[0]] = max(d.get(tok[0], 0), tok[1])
        for r in reads:
            for t in lastw.get(r, []):
                put(t)
        for w in writes:
            for t in lastw.get(w, []) + reads_of.get(w, []):
                put(t)
        for b in banks:
            if b in bank_of and bank_of[b][0] != e:
                put(bank_of[b][1])
        need(e, d.items())

    def done(e, tok, reads, writes, banks):
        know[tok] = dict(seen[e])
        for r in reads:
            reads_of.setdefault(r, []).append(tok)
        for w in writes:
            lastw[w] = [tok]
            reads_of[w] = []
        for b in banks:
            bank_of[b] = (e, tok)

    def op(e, fn, reads=(), writes=(), banks=(), join=False):
        deps(e, reads, () if join else writes, banks)
        s = "q_" + e
        total[s] = total.get(s, 0) + 1
        fn().then_inc(T.sem[s], 1)
        done(e, (s, total[s]), reads, writes, banks)

    def dma(e, out, in_, sem, reads=(), writes=()):
        deps(e, reads, writes, ())
        total[sem] = total.get(sem, 0) + 16
        eng[e].dma_start(out, in_).then_inc(T.sem[sem], 16)
        done(e, (sem, total[sem]), reads, writes, ())

    def arrives(name, sem, n):
        lastw[name] = [(sem, n)]
        total[sem] = n

    peers = [r for r in range(4) if r != rank]
    peers.sort(key=lambda r: (not topo.same_plane(topo.chip(core), topo.chip(T.cores[r])), r ^ rank))

    def n_eng(r):
        return len(topo.engines(core, T.cores[r]))

    def dst(r):
        rid, pid, _ = topo.addr(T.cores[r])
        return DstId(rid=rid, pnc=pid)

    for r in peers:
        n = len(topo.engines(T.cores[r], core))
        arrives("fl%d" % r, "fl%d" % r, n)
        arrives("K%d" % r, "kk%d" % r, n)
        arrives("P%d" % r, "ps%d" % r, n)

    V, S, P = g.vector, g.scalar, g.tensor

    def mm(bank, c0, c1, lhs, rhs, a, z, reads, name, p0=0, p1=128, step=1):
        op("t", lambda: P.matmul(T["B%d" % bank][p0:p1, c0:c1:step], lhs, rhs, a, z), reads, [name], [bank], join=True)

    def select(out, in_, pattern, how, base, reads, writes, fill=0.0, step=-1):
        op("g", lambda: g.affine_select(out, in_, pattern, how, fill, base, step), reads, writes)

    def ramp(out, pattern, base, step, name):
        op("g", lambda: g.iota(out, pattern, base, step, allow_small_or_imprecise_dtypes=True), (), [name])

    dma("s", T.LM[0:2, 0:2], T.lim[:], "d_lim", (), ["LM"])
    dma("y", T.A0[:], T.at[0:1, :], "d_at0", (), ["A0"])
    dma("y", T.FK[:], T.fk[:], "d_fk", (), ["FK"])
    dma("y", T.ME[:, 0:16], T.me[0:1, 0:2048], "d_me", (), ["MEa"])
    dma("y", T.ME[:, 16:32], T.me[0:1, 2048:4096], "d_me", (), ["MEb"])

    def table(i):
        c, e, h, x = 4096 * (i % 2), i // 2 % 2, i // 4 % 2, i // 8
        p, s = 64 * e + 32 * h + 16 * x, 16384 * e + 8192 * h + c
        dma("y", T.Tab[p:p + 16, 8 + c:8 + c + 4096], T.at[:, s:s + 4096], "tb%d" % i, (), ["Tab%d" % i])

    cs, cv = 1024 + FILL_S, 1024 + FILL_S + 1024 * FILL_D
    ones = T.ONES[:, 0:128]
    op("v", lambda: V.memset(T.ONEF[:], 1.0), (), ["ONEF"])
    op("v", lambda: V.memset(T.win[:, 0:1024], 0.0), (), ["win0"])
    for k in range(FILL_D):
        c = cs + 1024 * k
        dma("y", T.win[:, c:c + 1024], T.win[:, 0:1024], "dz%d" % k, ["win0"], ["win%d" % (5 + k)])
    op("s", lambda: S.activation(T.win[:, 1024:2048], T.win[:, 0:1024], COPY), ["win0"], ["win1"])
    op("s", lambda: S.activation(T.win[:, 2048:4096], T.win[:, 0:2048], COPY), ["win0", "win1"], ["win2"])
    op("s", lambda: S.activation(T.win[:, 4096:cs], T.win[:, 0:cs - 4096], COPY), ["win0", "win1"], ["win3"])
    select(T.E2[0:2, :], T.ONEF[0:2, :], [[1, 2], [0, 64]], A.is_equal, 0, ["ONEF"], ["E2"])
    op("g", lambda: g.iota(T.J0[:], [[-8, 2], [-1, 2], [-2, 4]], 16, 1), (), ["J0"])
    op("g", lambda: g.iota(T.Tab[:, 0:8], [[0, 8]], 0, 0), (), ["TabZ"])
    op("g", lambda: g.iota(T.Tab[:, 8200:8208], [[0, 8]], 0, 0), (), ["TabY"])
    ramp(T.E[:, 0:1], [[0, 1]], 0, 0, "E0")
    ramp(T.SH[:, 0:8], [[0, 8]], 0, 0, "SHz")
    op("v", lambda: V.tensor_copy(T.LMF[0:2, 0:2], T.LM[0:2, 0:2]), ["LM"], ["LMF"])
    mm(5, 0, 2, T.E2[0:2, :], T.LMF[0:2, 0:2], True, True, ["E2", "LMF"], "LH")
    op("v", lambda: V.memset(T.ONES[:], 1.0), (), ["ONES"])
    op("v", lambda: V.tensor_scalar(T.B0[:, 0:256], T.A0[:], T.B5[:, 0:1], T.B5[:, 1:2], A.max, A.min),
       ["A0", "LH"], ["clamp"], [0, 5])
    op("v", lambda: V.tensor_tensor(T.FL[:], T.A0[:], T.B0[:, 0:256], A.not_equal), ["A0", "clamp"], ["FL"], [0])

    mask = topo.mask(core, T.cores[peers[0]])

    def send_all(src, dsts, sem, local):
        g.remote_dma_fused([RemoteDMATransfer(dst_ids=[dst(r) for r in peers], dma_engine_mask=mask, remote_sem=T.sem[sem],
                                              srcs=[src], dsts=dsts)], local_sem=T.sem[local])
        total[local] = n_eng(peers[0])
    deps("g", ["FL"])
    send_all(T.FL[:], [T.fl[rank] for r in peers], "fl%d" % rank, "lf")
    g.sem_inc(T.sem.gi, 1)
    total["gi"] = 1

    for b in range(2):
        select(T.SH[:, 8 + 128 * b:136 + 128 * b], ones, [[2, 8], [16, 16]], A.is_equal, b, ["ONES"], ["SH%d" % b])
    select(T.LT[:], ones, [[1, 8], [8, 16]], A.is_gt, 0, ["ONES"], ["LT"])
    select(T.LE[:], ones, [[1, 8], [8, 16]], A.is_ge, 0, ["ONES"], ["LE"])
    select(T.PM[:], T.ONEF[:], [[1, 8], [8, 16]], A.is_equal, 0, ["ONEF"], ["PM"])
    ramp(T.DD[:], [[1, 2], [256, 16]], 1024, 2, "DD")
    ramp(T.SC[:, 0:1024], [[0, 1024]], 0, 0, "SC")
    select(T.IDN[:], ones, [[1, 128]], A.is_equal, 0, ["ONES"], ["IDN"])
    ramp(T.HM[:], [[0, 2], [-64, 2], [0, 32]], 0, 0, "HM")
    ramp(T.CT[:, 0:1], [[0, 1]], 0, 0, "CTz")
    for h in range(2):
        for b in range(2):
            n = "SE%d" % (2 * h + b)
            select(T[n][:], ones, [[2, 8], [32, 16]], A.is_equal, 16 * h + b, ["ONES"], [n])
    for q in range(4):
        n = "KH%d" % q
        select(T[n][:], T.ONES[:, 0:64], [[0, 2], [64, 2], [1, 16]], A.is_equal, 16 * q, ["ONES"], [n])
    select(T.SMA[:], T.ONEF[:, 0:32], [[1, 16], [16, 2]], A.is_equal, 0, ["ONEF"], ["SMA"])
    for b in (32, 64, 96):
        select(T.SMA[:], T.SMA[:], [[1, 16], [16, 2]], A.not_equal, b, ["SMA"], ["SMA"], 1.0)
    select(T.PERM[:], T.ONEF[:], [[1, 16], [16, 8]], A.is_equal, 0, ["ONEF"], ["PERM"])
    select(T.Z[:], T.ONES[:, 0:136], [[0, 17], [1, 8]], A.is_equal, -7, ["ONES"], ["Z"], step=0)

    op("v", lambda: V.memset(T.win[:, cv:16384], 0.0), (), ["win4"])
    op("v", lambda: V.tensor_scalar(T.B6[:, 0:256], T.FK[:], 8, None, A.add), ["FK"], ["K8"], [6])
    op("s", lambda: S.activation(T.HB[:], T.B6[:, 0:256], COPY), ["K8"], ["HB"], [6])
    op("v", lambda: V.tensor_copy(T.FKU[:], T.FK[:]), ["FK"], ["FKU"])
    op("v", lambda: V.tensor_scalar(T.J[:], T.J0[:], 15, None, A.bitwise_and), ["J0"], ["J"])
    op("v", lambda: V.tensor_tensor(T.LOB[:], T.B6[:, 0:256], T.HB[:], A.subtract), ["K8", "HB"], ["LOB"], [6])
    op("v", lambda: V.tensor_scalar(T.SELB[:, 0:1], T.J[:, 0:1], 0, 8192, A.is_equal, A.mult), ["J"], ["SELB"])
    op("v", lambda: V.tensor_scalar(T.SELP[:], T.J[:], 0, None, A.is_equal), ["J"], ["SELP"])
    for b in range(2):
        c, n = 256 * b, ["SHz", "SH0", "SH1"]
        mm(1, c, c + 256, T.SH[:, 8 + 128 * b:136 + 128 * b], T.HB[:], True, False, n + ["HB"], "Xp")
        mm(1, c, c + 256, T.SH[:, 128 * b:128 + 128 * b], T.LOB[:], False, True, n + ["LOB"], "Xp")

    need("y", [("gi", 1)])
    for i in range(EARLY):
        table(i)
    wins = ["win%d" % i for i in range(5 + FILL_D)]
    for r in [rank] + peers:
        deps("y", wins)
        src, name = (T.FL[:], "FL") if r == rank else (T.fl[r], "fl%d" % r)
        dma("y", T.win[32 * r:32 * r + 32:16, :], src, "rl%d" % r, [name], ["wr%d" % r])
    wr = ["wr%d" % r for r in range(4)]
    for i in range(EARLY, 16):
        if i >= EARLY + 5:
            deps("y", ["Tab%d" % (i - 5)])
        table(i)

    chunks = [(0, 2), (8, 2), (2, 2), (10, 2), (4, 2), (12, 2), (6, 1), (14, 1), (7, 1), (15, 1)]
    for u, n in chunks:
        o, off = T.G[:, 256 * u:256 * (u + n)], T.FKU[:, 16 * u:16 * (u + n)]
        if u < 8:
            op("v", lambda: V.tensor_copy(o, T.win[:, 0:16384].indirect(off)), wr + wins + ["FKU"], ["Gf%d" % u])
        else:
            op("s", lambda: S.activation(o, T.win[:, 0:16384].indirect(off), COPY), wr + wins + ["FKU"], ["Gf%d" % u])
    for u0, n in chunks:
        for u in range(u0, u0 + n):
            for b in range(2):
                mm(0, 16 * b + u, 16 * b + u + 1, T.G[:, 256 * u + b:256 * u + 256:2], T.SELB[:, 0:1], True, True,
                   ["Gf%d" % u0, "SELB"], "CNT")
    op("v", lambda: V.tensor_copy(T.MB[:, 0:32], T.ME[:]), ["MEa", "MEb"], ["MB0"])
    op("v", lambda: V.tensor_scalar(T.SV[:], T.B0[:, 0:32], 0, None, A.is_equal), ["CNT"], ["SV"], [0])
    op("v", lambda: V.tensor_tensor(T.NS[:], T.B0[:, 0:32], T.DD[:], A.min), ["CNT", "DD"], ["NS"], [0])
    op("v", lambda: V.tensor_tensor_scan(T.E[:, 1:17], T.SV[:, 0:16], T.SV[:, 16:32], 0.0, A.add, A.add), ["SV"], ["E"])
    op("v", lambda: V.tensor_tensor(T.MR[:], T.ME[:], T.MB[:, 0:32], A.subtract), ["MEa", "MEb", "MB0"], ["MR"])
    op("s", lambda: S.activation(T.X[:], T.B1[:], COPY), ["Xp"], ["X"], [1])
    sv0, sv1, ee = T.SV[:, 0:16], T.SV[:, 16:32], T.E[:, 0:16]
    mm(3, 0, 32, T.LT[:], T.SV[:], True, False, ["LT", "SV"], "WA")
    mm(3, 0, 16, T.LT[:], sv1, False, False, ["LT", "SV"], "WA")
    mm(3, 16, 32, T.LE[:], sv0, False, False, ["LE", "SV"], "WA")
    mm(3, 0, 32, T.PM[:], T.NS[:], False, False, ["PM", "NS"], "WA")
    mm(3, 0, 16, ones, ee, False, False, ["ONES", "E", "E0"], "WA")
    mm(3, 16, 32, ones, ee, False, True, ["ONES", "E", "E0"], "WA")
    op("v", lambda: V.tensor_copy(T.MB[:, 32:64], T.MR[:]), ["MR"], ["MB1"])
    op("v", lambda: V.tensor_copy(T.POS[:], T.B3[:, 0:32]), ["WA"], ["POS"], [3])
    op("v", lambda: V.tensor_tensor(T.MB[:, 64:96], T.MR[:], T.MB[:, 32:64], A.subtract), ["MR", "MB1"], ["MB2"])

    op("v", lambda: V.tensor_copy(T.SC[:].indirect(T.POS[:]), T.X[:]), ["POS", "X"], ["SC"])
    mm(4, 64, 65, ones, T.E[:, 16:17], True, True, ["ONES", "E"], "CN")
    mm(6, 128, 256, T.MB[:], T.IDN[:], True, True, ["MB0", "MB1", "MB2", "IDN"], "MTp", 0, 96)
    op("s", lambda: S.activation(T.MT[0:96, :], T.B6[0:96, 128:256], COPY), ["MTp"], ["MT"], [6])
    op("t", lambda: P.matmul(T.B7[:, 0:4], T.HM[:], ones, True, False), ["HM", "ONES"], ["KL"], [7], join=True)
    for i in range(4):
        h, b = i // 2, i % 2
        c = 256 * b + 128 * h
        mm(2, c, c + 128, T["SE%d" % i][0:96, :], T.MT[0:96, :], True, True, ["SE%d" % i, "MT"], "XMp")
    op("s", lambda: S.activation(T.XM[:], T.B2[:], COPY), ["XMp"], ["XM"], [2])
    op("s", lambda: S.activation(T.CT[:, 1:2], T.B4[:, 64:65], COPY), ["CN"], ["CT"], [4])
    dma("y", T.y[:, 1023:1025], T.CT[0:16, :], "d_ct", ["CT", "CTz"], ["yct"])
    for t in range(8):
        mm(5, t, 128, T.SC[:, t:1024:8], T.SELP[:], True, True, ["SC", "SELP"], "KT", step=8)
    op("v", lambda: V.tensor_copy(T.KB[:], T.B5[:, 0:128]), ["KT"], ["KB"], [5])
    for q in range(4):
        for e in range(2):
            for p in range(2):
                c = 64 * p + 32 * e
                op("t", lambda: P.matmul(T.B7[64 * e:64 * e + 64, q], T["KH%d" % q][:], T.KB[:, c:c + 32], False, q == 3 and p == 1),
                   ["KH%d" % q, "KB"], ["KL"], [7], join=True)
    op("v", lambda: V.memset(T.SCM[:, 0:1024], 0.0), (), ["SCM"])

    def send(r, out, in_, sem, local):
        rid, pid, _ = topo.addr(T.cores[r])
        g.remote_dma(out, in_, T.sem[sem], T.sem[local], pid, rid, topo.mask(core, T.cores[r]))
        total[local] = total.get(local, 0) + n_eng(r)
    for r in peers + [rank]:
        op("v", lambda: V.tensor_scalar(T.KS[:, 32 * r:32 * r + 32], T.B7[:, 0:4, r, :], 0, 8200, A.max, A.min), ["KL"], ["KS%d" % r], [7])
        if r != rank:
            deps("g", ["KS%d" % r])
            send(r, T["K%d" % rank][:], T.KS[:, 32 * r:32 * r + 32], "kk%d" % rank, "lk")

    def measures(b):
        op("v", lambda: V.tensor_copy(T.SCM[:].indirect(T.POS[:, 16 * b:16 * b + 16]), T.XM[:, 256 * b:256 * b + 256]),
           ["POS", "XM"], ["SCM"])
    measures(0)

    tabs = ["TabZ", "TabY"] + ["Tab%d" % i for i in range(16)]
    es_bank = {rank: 3, peers[0]: 4, peers[1]: 1, peers[2]: 5}

    def pick(r, q):
        lst, name, c = (T.KS, "KS%d" % r, 32 * r) if r == rank else (T["K%d" % r], "K%d" % r, 0)
        off = lst[:, c + 8 * q:c + 8 * q + 8]
        o = T["G%d" % r][:, 128 * q:128 * q + 128]
        if q < 2:
            op("v", lambda: V.tensor_copy(o, T.Tab[:, 0:8208].indirect(off)), tabs + [name], ["GA%d%d" % (r, q)])
        else:
            op("s", lambda: S.activation(o, T.Tab[:, 0:8208].indirect(off), COPY), tabs + [name], ["GA%d%d" % (r, q)])

    def add(r):
        for q in (0, 2, 1, 3):
            mm(es_bank[r], 128 + q, 256, T["G%d" % r][:, 128 * q:128 * q + 128], T.SMA[:], True, True,
               ["SMA", "GA%d%d" % (r, q)], "ES%d" % r, step=4)

    def sums(r, e):
        o = T["B%d" % es_bank[r]][:, 128:256]
        if e == "v":
            op("v", lambda: V.tensor_copy(T["R%d" % r][:], o), ["ES%d" % r], ["RS%d" % r], [es_bank[r]])
        else:
            op("s", lambda: S.activation(T["R%d" % r][:], o, COPY), ["ES%d" % r], ["RS%d" % r], [es_bank[r]])

    p0, p1, p2 = peers
    for r in peers + [rank]:
        pick(r, 0)
        pick(r, 1)
    for r in (p0, p1):
        pick(r, 2)
        pick(r, 3)
        add(r)
    sums(p0, "s")
    pick(p2, 2)
    pick(p2, 3)
    add(p2)
    sums(p1, "s")
    pick(rank, 2)
    pick(rank, 3)
    sums(p2, "s")
    add(rank)
    measures(1)
    for r in peers:
        deps("g", ["RS%d" % r])
        send(r, T["P%d" % rank][:], T["R%d" % r][:], "ps%d" % rank, "lp")

    for b in range(8):
        mm(2, 0, 128, T.Z[:, 7 - b:135 - b], T.SCM[:, 128 * b:128 * b + 128], b == 0, False, ["Z", "SCM"], "SUM")
    own = T["B%d" % es_bank[rank]][:, 128:256]
    op("v", lambda: V.tensor_tensor(T.B0[:, 256:384], T["P%d" % p0][:], own, A.add), ["P%d" % p0, "ES%d" % rank], ["Q0"],
       [0, es_bank[rank]])
    op("v", lambda: V.tensor_tensor(T["R%d" % rank][:], T["P%d" % p1][:], T.B0[:, 256:384], A.add), ["P%d" % p1, "Q0"],
       ["Q1"], [0])
    mm(2, 0, 128, T["R%d" % rank][:], T.PERM[:], False, False, ["Q1", "PERM"], "SUM")
    mm(2, 0, 128, T["P%d" % p2][:], T.PERM[:], False, True, ["P%d" % p2, "PERM"], "SUM")
    op("v", lambda: V.tensor_copy(T.YF[:], T.B2[:, 0:128]), ["SUM"], ["F"], [2])
    deps("y", ["yct"])
    dma("y", T.y[:, 0:1024], T.YF[:], "d_y", ["F"], ["y"])
    need("g", list(total.items()))
